import numpy as np
import ml_dtypes


def mxq(x, axis, fmt="e4m3"):
    dtype, down = {"e4m3": (ml_dtypes.float8_e4m3fn, 7), "e5m2": (ml_dtypes.float8_e5m2, 14)}[fmt]
    v = np.moveaxis(np.asarray(x, np.float32).astype(ml_dtypes.bfloat16).astype(np.float64), axis, -1)
    blocks = v.reshape(v.shape[:-1] + (-1, 32))
    amax = np.abs(blocks).max(-1, keepdims=True)
    byte = np.maximum(np.where(amax > 0, np.frexp(amax)[1] - 1 + 127, 0) - down, 1)
    scale = np.exp2(byte - 127.0)
    codes = (blocks / scale).astype(np.float32).astype(dtype).astype(np.float64)
    return np.moveaxis((codes * scale).reshape(v.shape), -1, axis)


WIDE = False


def mx_kscale(k):
    if not WIDE:
        return np.ones(k)
    levels = np.array([10, -10, 5, -5, 0])
    if k % 512:
        return np.exp2(np.random.permutation(np.resize(levels, k // 32))).repeat(32)
    a = np.empty((k // 512, 16))
    for p in range(k // 512):
        a[p, :8] = np.random.permutation(np.resize(levels, 8))
        for g in range(8):
            far = levels[np.abs(levels - a[p, g]) >= 10]
            a[p, g + 8] = far[np.random.randint(len(far))]
    return np.exp2(a.ravel()).repeat(32)


def f64(x):
    return np.asarray(x).astype(np.float64)


def striped(idx):
    return np.tile(idx.reshape(-1, 16).T, (8, 1)).astype(np.uint16)


def unstriped(offs):
    return offs[:16].T.reshape(-1).astype(np.int64)


def pack_weight(w):
    k, n = w.shape
    w = f64(np.asarray(w, np.float32).astype(ml_dtypes.bfloat16)).reshape(k // 32, 32, n)
    amax = np.abs(w).max(1)
    byte = np.clip(np.where(amax > 0, np.frexp(amax)[1] - 1 + 127 - 7, 1), 1, 254)
    scaled = (w * np.exp2(127.0 - byte)[:, None, :]).reshape(k, n).astype(np.float32)
    words = np.ascontiguousarray(scaled.reshape(k // 512, 128, 4, n).transpose(0, 1, 3, 2)).astype(ml_dtypes.float8_e4m3fn).view(np.uint8)
    return words, np.ascontiguousarray(byte.astype(np.uint8).reshape(k // 512, 16, n))


def unpack_weight(words, scales):
    g, p, n, _ = words.shape
    vals = np.ascontiguousarray(words).view(ml_dtypes.float8_e4m3fn).astype(np.float64) * np.repeat(np.exp2(scales.astype(np.float64) - 127.0), 8, axis=1)[..., None]
    return vals.transpose(0, 1, 3, 2).reshape(g * 512, n)


E2M1 = np.array([0.0, 0.5, 1.0, 1.5, 2.0, 3.0, 4.0, 6.0, -0.0, -0.5, -1.0, -1.5, -2.0, -3.0, -4.0, -6.0])


def pack_fp4(w):
    k, n = w.shape
    w = f64(np.asarray(w, np.float32).astype(ml_dtypes.bfloat16)).reshape(k // 32, 32, n)
    amax = np.abs(w).max(1)
    mant, ex = np.frexp(amax / 6.0)
    byte = np.clip(np.where(amax > 0, np.where(mant > 0.5, ex, ex - 1) + 127, 1), 1, 254)
    scaled = (w * np.exp2(127.0 - byte)[:, None, :]).reshape(k, n).astype(np.float32)
    c = np.ascontiguousarray(scaled.reshape(k // 512, 128, 4, n).transpose(0, 1, 3, 2)).astype(ml_dtypes.float4_e2m1fn).view(np.uint8) & 0xF
    words = (c[..., 0::2] | (c[..., 1::2] << 4)).reshape(k // 512, 128, 2 * n)
    return np.ascontiguousarray(words), np.ascontiguousarray(byte.astype(np.uint8).reshape(k // 512, 16, n))


def unpack_fp4(words, scales):
    g, _, n = scales.shape
    words = np.ascontiguousarray(words).reshape(g, 128, n, 2)
    nib = np.empty((g, 128, n, 4), np.uint8)
    nib[..., 0::2] = words & 0xF
    nib[..., 1::2] = words >> 4
    vals = E2M1[nib] * np.repeat(np.exp2(scales.astype(np.float64) - 127.0), 8, axis=1)[..., None]
    return vals.transpose(0, 1, 3, 2).reshape(g * 512, n)


def relu(v):
    return np.maximum(v, 0.0)


K, T, S, D, N, H = 1024, 2048, 512, 4, 256, 512


def setup_inputs():
    n = np.random.standard_normal
    s = mx_kscale(K)[:, None]
    u = mx_kscale(H)
    packed_xT = pack_weight(n((K, T)) * s)
    packed_w1 = pack_fp4(n((K, H)) / np.sqrt(K) / s)
    packed_w2 = pack_fp4(n((K, H)) / np.sqrt(K) / s)
    packed_w3 = pack_fp4(n((H, N)) / np.sqrt(H) / u[:, None])
    return {
        "x_words": packed_xT[0],
        "x_scales": packed_xT[1],
        "w1_words": packed_w1[0],
        "w1_scales": packed_w1[1],
        "w2_words": packed_w2[0],
        "w2_scales": packed_w2[1],
        "sat": (np.random.uniform(0.5, 1.2, (H, S))).astype(np.float32),
        "unit": (np.random.uniform(0.6, 1.4, (H, 1)) * u[:, None]).astype(np.float32),
        "w3_words": packed_w3[0],
        "w3_scales": packed_w3[1],
        "offs": striped(np.random.permutation(T)[:S]),
        "dsn": striped(np.random.permutation(S)),
    }


def reference(x_words, x_scales, w1_words, w1_scales, w2_words, w2_scales, sat, unit, w3_words, w3_scales, offs, dsn):
    xq = unpack_weight(x_words, x_scales)[:, unstriped(offs)]
    qe = unpack_fp4(w1_words, w1_scales).T @ xq
    queue = np.log(np.exp(qe) + 1.0)
    qd = queue[:, unstriped(dsn)]
    pres = queue - (0.8 * qd)
    ps_ = relu(pres) * f64(sat)
    phase = ps_.reshape(len(ps_), -1, D).sum(axis=2)
    green = phase / (phase + 1.5)
    oc = unpack_fp4(w2_words, w2_scales).T @ xq
    occ = np.log(np.exp(oc) + 1.0)
    serv = np.minimum(queue, 1.2 * (np.repeat(green, D, axis=1) * occ))
    sd = serv[:, unstriped(dsn)]
    qnew = queue - serv + 0.5 * sd
    hid = f64(unit) * (np.repeat(green, D, axis=1) * qnew + pres)
    return unpack_fp4(w3_words, w3_scales).T @ mxq(hid, 0, "e4m3")

from contextlib import ExitStack

import concourse.mybir as mybir
from concourse.masks import make_identity

F32 = mybir.dt.float32
BF16 = mybir.dt.bfloat16
I32 = mybir.dt.int32
U32 = mybir.dt.uint32
U16 = mybir.dt.uint16
U8 = mybir.dt.uint8
FP8X4 = mybir.dt.float8_e4m3fn_x4
FP4X4 = mybir.dt.float4_e2m1fn_x4
ACT = mybir.ActivationFunctionType
ALU = mybir.AluOpType

K, T, S, D, N, H = 1024, 2048, 512, 4, 256, 512
P = 128
PACK = 4
PASSES = K // (P * PACK)
V = S // D
HALF = S // 2
SLIVER = 16
FLOPS = 2 * S * (2 * K * H + H * N)


def tile_picked_ytraffs_green_p_kernel(tc, x_words, x_scales, w1_words, w1_scales, w2_words, w2_scales, sat, unit, w3_words, w3_scales, offs, dsn, out):
    nc = tc.nc
    with ExitStack() as ctx:
        lists = ctx.enter_context(tc.tile_pool(name="lists", bufs=1))
        keep = ctx.enter_context(tc.tile_pool(name="keep", bufs=1))
        psum = ctx.enter_context(tc.psum_pool(name="psum", bufs=1))

        def bank(b, name):
            return psum.tile([P, S], F32, tag="bank%d" % b, name=name)

        def load_scale_rows(queue, plane, scales):
            for quad in range(4):
                queue.dma_start(plane[32 * quad : 32 * quad + 4].bitcast(I32), scales[:, 4 * quad : 4 * quad + 4, :].rearrange("g r c -> r g c").bitcast(I32))

        offs_t = lists.tile([P, S // 16], U16, name="offs_t")
        dsn_t = lists.tile([P, S // 16], U16, name="dsn_t")
        nc.sync.dma_start(offs_t[:], offs)
        nc.sync.dma_start(dsn_t[:], dsn)

        xs = keep.tile([P, PASSES, T], U8, name="xs")
        nc.vector.memset(xs[:].rearrange("p g c -> p (g c)").bitcast(I32), 0)
        load_scale_rows(nc.scalar, xs, x_scales)

        raw_words = [keep.tile([P, PASSES, 2 * H], U8, name="raw_words%d" % w, tag="rw%d" % w, align_bytes=64) for w in range(2)]
        raw_scales = [keep.tile([P, PASSES, H], U8, name="raw_scales%d" % w, tag="rs%d" % w, align_bytes=64) for w in range(2)]
        nc.gpsimd.memset(raw_scales[0][:].rearrange("p g c -> p (g c)").bitcast(I32), 0)
        load_scale_rows(nc.gpsimd, raw_scales[0], w1_scales)
        u = keep.tile([P, PACK], F32, name="u")
        nc.gpsimd.dma_start(u[:], unit.rearrange("(p t) o -> p (t o)", t=PACK))

        xw = [keep.tile([P, T], U32, name="xw%d" % g, tag="big%d" % g) for g in range(PASSES)]
        nc.sync.dma_start(raw_words[0][:].bitcast(I32), w1_words.rearrange("g p c -> p g c").bitcast(I32))
        for g in range(PASSES):
            nc.sync.dma_start(xw[g][:].bitcast(I32), x_words[g].rearrange("p n r -> p (n r)").bitcast(I32))
        nc.sync.dma_start(raw_words[1][:].bitcast(I32), w2_words.rearrange("g p c -> p g c").bitcast(I32))
        nc.vector.memset(raw_scales[1][:].rearrange("p g c -> p (g c)").bitcast(I32), 0)
        load_scale_rows(nc.sync, raw_scales[1], w2_scales)

        ident = keep.tile([P, P], F32, name="ident")
        make_identity(nc, ident[:])
        offset = keep.tile([P, P], F32, name="offset")
        nc.gpsimd.memset(offset[:], 1.5)
        tiny = keep.tile([P, 1], F32, name="tiny")
        nc.gpsimd.memset(tiny[:], 2.0 ** -62)

        words = [keep.tile([P, PASSES, PACK, 2 * P], U8, name="words%d" % w, align_bytes=64) for w in range(2)]
        planes = [keep.tile([P, PASSES, PACK, P], U8, name="planes%d" % w, align_bytes=64) for w in range(2)]

        def deal_words(w):
            nc.vector.tensor_copy(words[w][:].bitcast(U16), raw_words[w][:].bitcast(U16).rearrange("p g (m t) -> p g t m", t=PACK))

        def deal_scales(w):
            nc.vector.tensor_copy(planes[w][:], raw_scales[w][:].rearrange("p g (m t) -> p g t m", t=PACK))

        gw = [keep.tile([P, S], U32, name="gw%d" % g, align_bytes=64) for g in range(PASSES)]
        gs = [keep.tile([P, S], U8, name="gs%d" % g, align_bytes=64) for g in range(PASSES)]
        deal_words(0)
        for g in range(PASSES):
            nc.vector.tensor_copy(gs[g][:], xs[:, g, :].indirect(offs_t[:]))
        nc.vector.tensor_copy(gw[0][:], xw[0][:].indirect(offs_t[:]))
        deal_scales(0)
        nc.vector.tensor_copy(gw[1][:], xw[1][:].indirect(offs_t[:]))
        deal_words(1)
        deal_scales(1)

        sat_t = keep.tile([P, PACK, S], F32, name="sat_t", tag="big0")
        nc.sync.dma_start(sat_t[:], sat.rearrange("(p t) j -> p t j", t=PACK))

        w3w = keep.tile([P, 2 * N], U8, name="w3w", tag="rw0", align_bytes=64)
        nc.sync.dma_start(w3w[:].bitcast(I32), w3_words[0].bitcast(I32))
        w3s = keep.tile([P, 1, N], U8, name="w3s", tag="rs0", align_bytes=64)
        nc.gpsimd.memset(w3s[:].rearrange("p g c -> p (g c)").bitcast(I32), 0)
        load_scale_rows(nc.sync, w3s, w3_scales)

        pre = {}

        def product(w, t, g):
            if g == 0:
                pre[w, t] = bank(PACK * w + t, "pre%d%d" % (w, t))
            nc.tensor.matmul_mx(pre[w, t][:], lhsT=words[w][:, g, t, :].bitcast(FP4X4), lhsT_scale=planes[w][:, g, t, :],
                                rhs=gw[g][:].bitcast(FP8X4), rhs_scale=gs[g][:], start=(g == 0), stop=(g == PASSES - 1))

        ln_order = [(0, 0)]
        for t in range(1, PACK):
            ln_order.extend([(0, t), (1, t - 1)])
        ln_order.append((1, PACK - 1))
        slot = {key: (k + 1) % len(ln_order) for k, key in enumerate(ln_order)}
        sig = keep.tile([P, len(ln_order) * S], F32, name="sig")
        ends = keep.tile([P, 2 * S], F32, name="ends")

        def sigmoid(w, t):
            c = slot[w, t] * S
            nc.scalar.activation(sig[:, c : c + S], pre[w, t][:], ACT.Sigmoid, scale=-1.0)

        for g in range(PASSES):
            for t in range(PACK):
                product(0, t, g)
        for t in range(PACK):
            sigmoid(0, t)
        for t in range(PACK):
            for g in range(PASSES):
                product(1, t, g)
            sigmoid(1, t)

        def log_of(w, t):
            c = slot[w, t] * S
            if (w, t) == ln_order[0]:
                nc.scalar.activation(ends[:, S - SLIVER :], sig[:, S - SLIVER : 2 * S], ACT.Ln, bias=tiny[:])
                return ends[:, S:]
            if (w, t) == ln_order[-1]:
                nc.scalar.activation(ends[:, : S - SLIVER], sig[:, : S - SLIVER], ACT.Ln, bias=tiny[:])
                return ends[:, :S]
            nc.scalar.activation(sig[:, c - S : c], sig[:, c : c + S], ACT.Ln, bias=tiny[:])
            return sig[:, c - S : c]

        def rows(name):
            return [keep.tile([P, S], F32, name="%s%d" % (name, t)) for t in range(PACK)]

        queue, down, pres, ps, occ, flow, nserv, back, turned = [rows(n) for n in ("queue", "down", "pres", "ps", "occ", "flow", "nserv", "back", "turned")]
        recip = [keep.tile([P, V], F32, name="recip%d" % t) for t in range(PACK)]
        green = [keep.tile([P, V], F32, name="green%d" % t) for t in range(PACK)]
        held = keep.tile([P, PACK, S], F32, name="held")
        moved = keep.tile([P, PACK, S], F32, name="moved")
        small, sums = {}, {}

        def by_phase(ap):
            return ap.rearrange("p (v d) -> p v d", d=D)

        def spread(t):
            return green[t][:].unsqueeze(2).to_broadcast([P, V, D])

        def fetch(dst, window, scale):
            for h in range(2):
                nc.scalar.activation(dst[:, h * HALF : (h + 1) * HALF], window[:].indirect(dsn_t[:, h * 16 : (h + 1) * 16]), ACT.Copy, scale=scale)

        def turn(dst, src, start, stop):
            nc.tensor.matmul(dst, lhsT=src, rhs=ident[:], start=start, stop=stop, is_transpose=True)

        def turn_rows(dst, src, start, stop):
            for b in range(PACK):
                turn(dst[:, b * P : (b + 1) * P], src[:, b * P : (b + 1) * P], start and b == 0, stop and b == PACK - 1)

        def stage_queue(t):
            nc.vector.scalar_tensor_tensor(queue[t][:], log_of(0, t), -1.0, pre[0, t][:], ALU.mult, ALU.max)

        def stage_pressure(t):
            fetch(down[t], queue[t], -0.8)
            nc.vector.tensor_tensor(pres[t][:], queue[t][:], down[t][:], ALU.add)
            nc.vector.scalar_tensor_tensor(ps[t][:], pres[t][:], 0.0, sat_t[:, t, :], ALU.max, ALU.mult)
            small[t] = bank(t, "small%d" % t)
            turn(small[t][:, :V], offset[:], True, False)
            for d in range(D):
                turn(small[t][:, :V], by_phase(ps[t][:])[:, :, d], False, d == D - 1)
            nc.vector.scalar_tensor_tensor(occ[t][:], log_of(1, t), -1.0, pre[1, t][:], ALU.mult, ALU.max)

        def stage_green(t):
            nc.vector.reciprocal(recip[t][:], small[t][:, :V])
            turn(small[t][:, V : 2 * V], recip[t][:], True, True)
            nc.scalar.activation(green[t][:], small[t][:, V : 2 * V], ACT.Copy, scale=-1.5, bias=1.0)
            nc.scalar.activation(held[:, t, :], pres[t][:], ACT.Copy, scale=u[:, t : t + 1])

        def stage_serve(t):
            nc.vector.scalar_tensor_tensor(by_phase(flow[t][:]), by_phase(occ[t][:]), -1.2, spread(t), ALU.mult, ALU.mult)
            nc.vector.scalar_tensor_tensor(nserv[t][:], queue[t][:], -1.0, flow[t][:], ALU.mult, ALU.max)
            fetch(back[t], nserv[t], -0.5)
            if t < PACK - 1:
                sums[t] = bank(PACK + t, "sums%d" % t)
                turn_rows(sums[t], queue[t], True, False)
                turn_rows(sums[t], nserv[t], False, False)
            else:
                nc.vector.tensor_tensor(turned[t][:], queue[t][:], nserv[t][:], ALU.add)

        def stage_update(t):
            if t < PACK - 1:
                turn_rows(sums[t], back[t], False, True)
                nc.scalar.copy(turned[t][:], sums[t][:])
                qnew = bank(t, "qnew%d" % t)
                turn_rows(qnew, turned[t], True, True)
            else:
                qnew = flow[t]
                nc.vector.tensor_tensor(qnew[:], turned[t][:], back[t][:], ALU.add)
            nc.vector.scalar_tensor_tensor(by_phase(moved[:, t, :]), by_phase(qnew[:]), u[:, t : t + 1], spread(t), ALU.mult, ALU.mult)

        stages = (stage_queue, stage_pressure, stage_green, stage_serve, stage_update)
        for step in range(PACK + len(stages) - 1):
            for k in range(len(stages)):
                if 0 <= step - k < PACK:
                    stages[k](step - k)

        acc = [bank(PACK + h, "acc%d" % h) for h in range(N // P)]
        res = keep.tile([P, N // P, S], F32, name="res")
        hid, codes, scales = [], [], []
        for c in range(2):
            cols = slice(c * HALF, (c + 1) * HALF)
            hid.append(keep.tile([P, HALF * PACK], BF16, name="hid%d" % c, align_bytes=64))
            nc.vector.tensor_tensor(hid[c][:].rearrange("p (c i t) -> p c t i", i=4, t=PACK),
                                    held[:, :, cols].rearrange("p t (c i) -> p c t i", i=4),
                                    moved[:, :, cols].rearrange("p t (c i) -> p c t i", i=4), ALU.add)
        for c in range(2):
            cols = slice(c * HALF, (c + 1) * HALF)
            codes = keep.tile([P, HALF], U32, name="codes%d" % c, align_bytes=64)
            plane = keep.tile([P, HALF], U8, name="plane%d" % c, align_bytes=64)
            nc.vector.quantize_mx(codes[:].bitcast(FP8X4), plane[:], hid[c][:])
            for h in range(N // P):
                nc.tensor.matmul_mx(acc[h][:, cols], lhsT=w3w[:, 2 * P * h : 2 * P * (h + 1)].bitcast(FP4X4), lhsT_scale=w3s[:, 0, P * h : P * (h + 1)],
                                    rhs=codes[:].bitcast(FP8X4), rhs_scale=plane[:], start=True, stop=True)
                nc.scalar.copy(res[:, h, cols], acc[h][:, cols])
            nc.sync.dma_start(out[:, cols].rearrange("(h p) j -> p h j", p=P), res[:, :, cols])
